import numpy as np
import ml_dtypes


def mxq(x, axis, fmt="e4m3"):
    dtype, down = {"e4m3": (ml_dtypes.float8_e4m3fn, 7), "e5m2": (ml_dtypes.float8_e5m2, 14)}[fmt]
    v = np.moveaxis(np.asarray(x, np.float32).astype(ml_dtypes.bfloat16).astype(np.float64), axis, -1)
    blocks = v.reshape(v.shape[:-1] + (-1, 32))
    amax = np.abs(blocks).max(-1, keepdims=True)
    byte = np.maximum(np.where(amax > 0, np.frexp(amax)[1] - 1 + 127, 0) - down, 1)
    scale = np.exp2(byte - 127.0)
    codes = (blocks / scale).astype(np.float32).astype(dtype).astype(np.float64)
    return np.moveaxis((codes * scale).reshape(v.shape), -1, axis)


WIDE = False


def mx_kscale(k):
    if not WIDE:
        return np.ones(k)
    levels = np.array([10, -10, 5, -5, 0])
    if k % 512:
        return np.exp2(np.random.permutation(np.resize(levels, k // 32))).repeat(32)
    a = np.empty((k // 512, 16))
    for p in range(k // 512):
        a[p, :8] = np.random.permutation(np.resize(levels, 8))
        for g in range(8):
            far = levels[np.abs(levels - a[p, g]) >= 10]
            a[p, g + 8] = far[np.random.randint(len(far))]
    return np.exp2(a.ravel()).repeat(32)


def f64(x):
    return np.asarray(x).astype(np.float64)


def striped(idx):
    return np.tile(np.asarray(idx).reshape(-1, 16).T, (8, 1)).astype(np.uint16)


def unstriped(offs):
    return offs[:16].T.reshape(-1).astype(np.int64)


B, N, T, D, DV, NQ = 1, 512, 1024, 256, 0, 512


def setup_inputs():
    n = np.random.standard_normal
    idx = np.random.permutation(T)[:B * N]
    z = mx_kscale(NQ)[:, None]
    return {
        "g": (n((B, NQ, N)) * z / np.sqrt(NQ)).astype(np.float32),
        "qm": (n((B, NQ, D)) / z).astype(np.float32),
        "offs": striped(idx),
    }


def reference(g, qm, offs):
    idx = unstriped(offs)
    dk = mxq(f64(qm), 1, "e4m3").transpose(0, 2, 1) @ mxq(f64(g), 1, "e4m3")
    out = np.zeros((D, T))
    out[:, idx] = dk.transpose(1, 0, 2).reshape(D, B * N)
    return out

@@ -1,0 +1,117 @@
+from contextlib import ExitStack
+
+import concourse.mybir as mybir
+
+F32 = mybir.dt.float32
+BF16 = mybir.dt.bfloat16
+U32 = mybir.dt.uint32
+U16 = mybir.dt.uint16
+U8 = mybir.dt.uint8
+FP8X4 = mybir.dt.float8_e4m3fn_x4
+
+P = 128
+PACK = 4
+NQ = 512
+SLOTS = 512
+D = 256
+T = 1024
+BLOCKS = D // P
+
+FLOPS = 2 * NQ * SLOTS * D
+
+
+CHUNKS = [128,128,256]
+
+
+def interleave(nc, grouped, raw, vector_cols, width):
+    for copy, a, b in ((nc.vector.tensor_copy, 0, vector_cols), (nc.scalar.copy, vector_cols, width)):
+        if b > a:
+            copy(
+                out=grouped[:, a:b, :].rearrange("p (c i) t -> p c t i", i=4),
+                in_=raw[:, :, a:b].rearrange("p t (c i) -> p c t i", i=4),
+            )
+
+
+def tile_attend_dk_kernel(tc, g, qm, offs, out):
+    nc = tc.nc
+    g_rows = g.rearrange("b (p t) n -> p (b t) n", t=PACK)
+    qm_rows = qm.rearrange("b (p t) d -> p (b t) d", t=PACK)
+    with ExitStack() as ctx:
+        held = ctx.enter_context(tc.tile_pool(name="held", bufs=1))
+        psum = ctx.enter_context(tc.psum_pool(name="psum", bufs=1))
+        offsets = held.tile([P, SLOTS // 16], U16, name="offsets")
+        warm = held.tile([P, 8], F32, name="warm")
+        q0_raw = held.tile([P, PACK, 128], F32, name="q0_raw")
+        q0_grp = held.tile([P, 128, PACK], BF16, name="q0_grp", align_bytes=64)
+        q0_codes = held.tile([P, 128], U32, name="q0_codes", align_bytes=64)
+        q0_scales = held.tile([P, 128], U8, name="q0_scales", align_bytes=64)
+        q1_raw = held.tile([P, PACK, 128], F32, name="q1_raw")
+        q1_grp = held.tile([P, 128, PACK], BF16, name="q1_grp", align_bytes=64)
+        q1_codes = held.tile([P, 128], U32, name="q1_codes", align_bytes=64)
+        q1_scales = held.tile([P, 128], U8, name="q1_scales", align_bytes=64)
+        g0_raw = held.tile([P, PACK, 128], F32, name="g0_raw")
+        g0_grp = held.tile([P, 128, PACK], BF16, name="g0_grp", align_bytes=64)
+        g0_codes = held.tile([P, 128], U32, name="g0_codes", align_bytes=64)
+        g0_scales = held.tile([P, 128], U8, name="g0_scales", align_bytes=64)
+        g1_raw = held.tile([P, PACK, 128], F32, name="g1_raw")
+        g1_grp = held.tile([P, 128, PACK], BF16, name="g1_grp", align_bytes=64)
+        g1_codes = held.tile([P, 128], U32, name="g1_codes", align_bytes=64)
+        g1_scales = held.tile([P, 128], U8, name="g1_scales", align_bytes=64)
+        g2_raw = held.tile([P, PACK, 256], F32, tag="late", name="g2_raw")
+        g2_grp = held.tile([P, 256, PACK], BF16, name="g2_grp", align_bytes=64)
+        g2_codes = held.tile([P, 256], U32, name="g2_codes", align_bytes=64)
+        g2_scales = held.tile([P, 256], U8, name="g2_scales", align_bytes=64)
+        nc.sync.dma_start(out=q0_raw[:], in_=qm_rows[:, :, 0 : 128])
+        nc.sync.dma_start(out=g0_raw[:], in_=g_rows[:, :, 0 : 128])
+        nc.sync.dma_start(out=q1_raw[:], in_=qm_rows[:, :, 128 : 256])
+        nc.sync.dma_start(out=g1_raw[:], in_=g_rows[:, :, 128 : 256])
+        nc.sync.dma_start(offsets[:], offs)
+        nc.sync.dma_start(out=g2_raw[:], in_=g_rows[:, :, 256 : 512])
+        win0 = held.tile([P, T], F32, name="win0")
+        win1 = held.tile([P, T], F32, name="win1")
+        nc.vector.memset(warm[:], 0.0)
+        nc.scalar.copy(out=warm[:, 4:8], in_=warm[:, 0:4])
+        nc.vector.memset(win0[:], 0.0)
+        nc.gpsimd.memset(win1[:], 0.0)
+        interleave(nc, q0_grp, q0_raw, 128, 128)
+        interleave(nc, g0_grp, g0_raw, 128, 128)
+        nc.vector.quantize_mx(out=q0_codes[:].bitcast(FP8X4), scales=q0_scales[:], in_=q0_grp[:].rearrange("p c t -> p (c t)"))
+        nc.vector.quantize_mx(out=g0_codes[:].bitcast(FP8X4), scales=g0_scales[:], in_=g0_grp[:].rearrange("p c t -> p (c t)"))
+        acc0_0 = psum.tile([P, 128], F32, name="acc0_0")
+        nc.tensor.matmul_mx(out=acc0_0[:], lhsT=q0_codes[:].bitcast(FP8X4), lhsT_scale=q0_scales[:], rhs=g0_codes[:].bitcast(FP8X4), rhs_scale=g0_scales[:], start=True, stop=True)
+        val0_0 = held.tile([P, 128], F32, name="val0_0")
+        nc.vector.tensor_copy(out=val0_0[:], in_=acc0_0[:])
+        interleave(nc, q1_grp, q1_raw, 0, 128)
+        nc.vector.quantize_mx(out=q1_codes[:].bitcast(FP8X4), scales=q1_scales[:], in_=q1_grp[:].rearrange("p c t -> p (c t)"))
+        acc1_0 = psum.tile([P, 128], F32, name="acc1_0")
+        nc.tensor.matmul_mx(out=acc1_0[:], lhsT=q1_codes[:].bitcast(FP8X4), lhsT_scale=q1_scales[:], rhs=g0_codes[:].bitcast(FP8X4), rhs_scale=g0_scales[:], start=True, stop=True)
+        val1_0 = held.tile([P, 128], F32, name="val1_0")
+        nc.scalar.copy(out=val1_0[:], in_=acc1_0[:])
+        interleave(nc, g1_grp, g1_raw, 128, 128)
+        nc.vector.quantize_mx(out=g1_codes[:].bitcast(FP8X4), scales=g1_scales[:], in_=g1_grp[:].rearrange("p c t -> p (c t)"))
+        acc0_1 = psum.tile([P, 128], F32, name="acc0_1")
+        nc.tensor.matmul_mx(out=acc0_1[:], lhsT=q0_codes[:].bitcast(FP8X4), lhsT_scale=q0_scales[:], rhs=g1_codes[:].bitcast(FP8X4), rhs_scale=g1_scales[:], start=True, stop=True)
+        val0_1 = held.tile([P, 128], F32, name="val0_1")
+        nc.scalar.copy(out=val0_1[:], in_=acc0_1[:])
+        interleave(nc, g2_grp, g2_raw, 0, 256)
+        nc.vector.quantize_mx(out=g2_codes[:].bitcast(FP8X4), scales=g2_scales[:], in_=g2_grp[:].rearrange("p c t -> p (c t)"))
+        acc1_1 = psum.tile([P, 128], F32, name="acc1_1")
+        nc.tensor.matmul_mx(out=acc1_1[:], lhsT=q1_codes[:].bitcast(FP8X4), lhsT_scale=q1_scales[:], rhs=g1_codes[:].bitcast(FP8X4), rhs_scale=g1_scales[:], start=True, stop=True)
+        val1_1 = held.tile([P, 128], F32, tag="late", name="val1_1")
+        nc.scalar.copy(out=val1_1[:], in_=acc1_1[:])
+        acc0_2 = psum.tile([P, 256], F32, name="acc0_2")
+        nc.tensor.matmul_mx(out=acc0_2[:], lhsT=q0_codes[:].bitcast(FP8X4), lhsT_scale=q0_scales[:], rhs=g2_codes[:].bitcast(FP8X4), rhs_scale=g2_scales[:], start=True, stop=True)
+        val0_2 = held.tile([P, 256], F32, name="val0_2")
+        nc.scalar.copy(out=val0_2[:], in_=acc0_2[:])
+        acc1_2 = psum.tile([P, 256], F32, name="acc1_2")
+        nc.tensor.matmul_mx(out=acc1_2[:], lhsT=q1_codes[:].bitcast(FP8X4), lhsT_scale=q1_scales[:], rhs=g2_codes[:].bitcast(FP8X4), rhs_scale=g2_scales[:], start=True, stop=True)
+        val1_2 = held.tile([P, 256], F32, name="val1_2")
+        nc.scalar.copy(out=val1_2[:], in_=acc1_2[:])
+        nc.vector.tensor_copy(win0[:].indirect(offsets[:, 0 : 8]), val0_0[:])
+        nc.vector.tensor_copy(win1[:].indirect(offsets[:, 0 : 8]), val1_0[:])
+        nc.vector.tensor_copy(win0[:].indirect(offsets[:, 8 : 16]), val0_1[:])
+        nc.vector.tensor_copy(win1[:].indirect(offsets[:, 8 : 16]), val1_1[:])
+        nc.vector.tensor_copy(win0[:].indirect(offsets[:, 16 : 32]), val0_2[:])
+        nc.sync.dma_start(out=out[0 : 128, :], in_=win0[:])
+        nc.vector.tensor_copy(win1[:].indirect(offsets[:, 16 : 32]), val1_2[:])
+        nc.sync.dma_start(out=out[128 : 256, :], in_=win1[:])

@@ -15,21 +15,31 @@ NQ = 512
 SLOTS = 512
 D = 256
 T = 1024
-BLOCKS = D // P
 
 FLOPS = 2 * NQ * SLOTS * D
 
 
-CHUNKS = [128,128,256]
+def interleave(copy, grouped, raw):
+    copy(
+        out=grouped.rearrange("p (c i) t -> p c t i", i=4),
+        in_=raw.rearrange("p t (c i) -> p c t i", i=4),
+    )
 
 
-def interleave(nc, grouped, raw, vector_cols, width):
-    for copy, a, b in ((nc.vector.tensor_copy, 0, vector_cols), (nc.scalar.copy, vector_cols, width)):
-        if b > a:
-            copy(
-                out=grouped[:, a:b, :].rearrange("p (c i) t -> p c t i", i=4),
-                in_=raw[:, :, a:b].rearrange("p t (c i) -> p c t i", i=4),
-            )
+def quantize(nc, codes, scales, grouped):
+    nc.vector.quantize_mx(out=codes.bitcast(FP8X4), scales=scales, in_=grouped.rearrange("p c t -> p (c t)"))
+
+
+def product(nc, acc, q_codes, q_scales, g_codes, g_scales):
+    nc.tensor.matmul_mx(
+        out=acc,
+        lhsT=q_codes.bitcast(FP8X4),
+        lhsT_scale=q_scales,
+        rhs=g_codes.bitcast(FP8X4),
+        rhs_scale=g_scales,
+        start=True,
+        stop=True,
+    )
 
 
 def tile_attend_dk_kernel(tc, g, qm, offs, out):
@@ -40,78 +50,88 @@ def tile_attend_dk_kernel(tc, g, qm, offs, out):
         held = ctx.enter_context(tc.tile_pool(name="held", bufs=1))
         psum = ctx.enter_context(tc.psum_pool(name="psum", bufs=1))
         offsets = held.tile([P, SLOTS // 16], U16, name="offsets")
-        warm = held.tile([P, 8], F32, name="warm")
-        q0_raw = held.tile([P, PACK, 128], F32, name="q0_raw")
-        q0_grp = held.tile([P, 128, PACK], BF16, name="q0_grp", align_bytes=64)
-        q0_codes = held.tile([P, 128], U32, name="q0_codes", align_bytes=64)
-        q0_scales = held.tile([P, 128], U8, name="q0_scales", align_bytes=64)
-        q1_raw = held.tile([P, PACK, 128], F32, name="q1_raw")
-        q1_grp = held.tile([P, 128, PACK], BF16, name="q1_grp", align_bytes=64)
-        q1_codes = held.tile([P, 128], U32, name="q1_codes", align_bytes=64)
-        q1_scales = held.tile([P, 128], U8, name="q1_scales", align_bytes=64)
-        g0_raw = held.tile([P, PACK, 128], F32, name="g0_raw")
-        g0_grp = held.tile([P, 128, PACK], BF16, name="g0_grp", align_bytes=64)
-        g0_codes = held.tile([P, 128], U32, name="g0_codes", align_bytes=64)
-        g0_scales = held.tile([P, 128], U8, name="g0_scales", align_bytes=64)
-        g1_raw = held.tile([P, PACK, 128], F32, name="g1_raw")
-        g1_grp = held.tile([P, 128, PACK], BF16, name="g1_grp", align_bytes=64)
-        g1_codes = held.tile([P, 128], U32, name="g1_codes", align_bytes=64)
-        g1_scales = held.tile([P, 128], U8, name="g1_scales", align_bytes=64)
-        g2_raw = held.tile([P, PACK, 256], F32, tag="late", name="g2_raw")
-        g2_grp = held.tile([P, 256, PACK], BF16, name="g2_grp", align_bytes=64)
-        g2_codes = held.tile([P, 256], U32, name="g2_codes", align_bytes=64)
-        g2_scales = held.tile([P, 256], U8, name="g2_scales", align_bytes=64)
-        nc.sync.dma_start(out=q0_raw[:], in_=qm_rows[:, :, 0 : 128])
-        nc.sync.dma_start(out=g0_raw[:], in_=g_rows[:, :, 0 : 128])
-        nc.sync.dma_start(out=q1_raw[:], in_=qm_rows[:, :, 128 : 256])
-        nc.sync.dma_start(out=g1_raw[:], in_=g_rows[:, :, 128 : 256])
-        nc.sync.dma_start(offsets[:], offs)
-        nc.sync.dma_start(out=g2_raw[:], in_=g_rows[:, :, 256 : 512])
+        V, S = nc.vector.tensor_copy, nc.scalar.copy
+
+        def raw_tile(name, width, tag=""):
+            return held.tile([P, PACK, width], F32, name=name + "_raw", tag=tag)
+
+        def grp_tile(name, width, tag=""):
+            return held.tile([P, width, PACK], BF16, name=name + "_grp", align_bytes=64, tag=tag)
+
+        def mx_tiles(name, width):
+            codes = held.tile([P, width], U32, name=name + "_codes", align_bytes=64)
+            scales = held.tile([P, width], U8, name=name + "_scales", align_bytes=64)
+            return codes, scales
+
+        def scatter(window, values, a, b):
+            nc.vector.tensor_copy(window[:].indirect(offsets[:, a // 16 : b // 16]), values)
+
+        q0_raw, q1_raw = raw_tile("q0", 128), raw_tile("q1", 128)
+        g0_raw, g1_raw, g2_raw, g3_raw = raw_tile("g0", 128), raw_tile("g1", 128), raw_tile("g2", 128), raw_tile("g3", 128)
+        q0c, q0s = mx_tiles("q0", 128)
+        q1c, q1s = mx_tiles("q1", 128)
+        gc, gs = mx_tiles("g", 512)
         win0 = held.tile([P, T], F32, name="win0")
         win1 = held.tile([P, T], F32, name="win1")
-        nc.vector.memset(warm[:], 0.0)
-        nc.scalar.copy(out=warm[:, 4:8], in_=warm[:, 0:4])
-        nc.vector.memset(win0[:], 0.0)
-        nc.gpsimd.memset(win1[:], 0.0)
-        interleave(nc, q0_grp, q0_raw, 128, 128)
-        interleave(nc, g0_grp, g0_raw, 128, 128)
-        nc.vector.quantize_mx(out=q0_codes[:].bitcast(FP8X4), scales=q0_scales[:], in_=q0_grp[:].rearrange("p c t -> p (c t)"))
-        nc.vector.quantize_mx(out=g0_codes[:].bitcast(FP8X4), scales=g0_scales[:], in_=g0_grp[:].rearrange("p c t -> p (c t)"))
-        acc0_0 = psum.tile([P, 128], F32, name="acc0_0")
-        nc.tensor.matmul_mx(out=acc0_0[:], lhsT=q0_codes[:].bitcast(FP8X4), lhsT_scale=q0_scales[:], rhs=g0_codes[:].bitcast(FP8X4), rhs_scale=g0_scales[:], start=True, stop=True)
-        val0_0 = held.tile([P, 128], F32, name="val0_0")
-        nc.vector.tensor_copy(out=val0_0[:], in_=acc0_0[:])
-        interleave(nc, q1_grp, q1_raw, 0, 128)
-        nc.vector.quantize_mx(out=q1_codes[:].bitcast(FP8X4), scales=q1_scales[:], in_=q1_grp[:].rearrange("p c t -> p (c t)"))
-        acc1_0 = psum.tile([P, 128], F32, name="acc1_0")
-        nc.tensor.matmul_mx(out=acc1_0[:], lhsT=q1_codes[:].bitcast(FP8X4), lhsT_scale=q1_scales[:], rhs=g0_codes[:].bitcast(FP8X4), rhs_scale=g0_scales[:], start=True, stop=True)
-        val1_0 = held.tile([P, 128], F32, name="val1_0")
-        nc.scalar.copy(out=val1_0[:], in_=acc1_0[:])
-        interleave(nc, g1_grp, g1_raw, 128, 128)
-        nc.vector.quantize_mx(out=g1_codes[:].bitcast(FP8X4), scales=g1_scales[:], in_=g1_grp[:].rearrange("p c t -> p (c t)"))
-        acc0_1 = psum.tile([P, 128], F32, name="acc0_1")
-        nc.tensor.matmul_mx(out=acc0_1[:], lhsT=q0_codes[:].bitcast(FP8X4), lhsT_scale=q0_scales[:], rhs=g1_codes[:].bitcast(FP8X4), rhs_scale=g1_scales[:], start=True, stop=True)
-        val0_1 = held.tile([P, 128], F32, name="val0_1")
-        nc.scalar.copy(out=val0_1[:], in_=acc0_1[:])
-        interleave(nc, g2_grp, g2_raw, 0, 256)
-        nc.vector.quantize_mx(out=g2_codes[:].bitcast(FP8X4), scales=g2_scales[:], in_=g2_grp[:].rearrange("p c t -> p (c t)"))
-        acc1_1 = psum.tile([P, 128], F32, name="acc1_1")
-        nc.tensor.matmul_mx(out=acc1_1[:], lhsT=q1_codes[:].bitcast(FP8X4), lhsT_scale=q1_scales[:], rhs=g1_codes[:].bitcast(FP8X4), rhs_scale=g1_scales[:], start=True, stop=True)
-        val1_1 = held.tile([P, 128], F32, tag="late", name="val1_1")
-        nc.scalar.copy(out=val1_1[:], in_=acc1_1[:])
-        acc0_2 = psum.tile([P, 256], F32, name="acc0_2")
-        nc.tensor.matmul_mx(out=acc0_2[:], lhsT=q0_codes[:].bitcast(FP8X4), lhsT_scale=q0_scales[:], rhs=g2_codes[:].bitcast(FP8X4), rhs_scale=g2_scales[:], start=True, stop=True)
-        val0_2 = held.tile([P, 256], F32, name="val0_2")
-        nc.scalar.copy(out=val0_2[:], in_=acc0_2[:])
-        acc1_2 = psum.tile([P, 256], F32, name="acc1_2")
-        nc.tensor.matmul_mx(out=acc1_2[:], lhsT=q1_codes[:].bitcast(FP8X4), lhsT_scale=q1_scales[:], rhs=g2_codes[:].bitcast(FP8X4), rhs_scale=g2_scales[:], start=True, stop=True)
-        val1_2 = held.tile([P, 256], F32, name="val1_2")
-        nc.scalar.copy(out=val1_2[:], in_=acc1_2[:])
-        nc.vector.tensor_copy(win0[:].indirect(offsets[:, 0 : 8]), val0_0[:])
-        nc.vector.tensor_copy(win1[:].indirect(offsets[:, 0 : 8]), val1_0[:])
-        nc.vector.tensor_copy(win0[:].indirect(offsets[:, 8 : 16]), val0_1[:])
-        nc.vector.tensor_copy(win1[:].indirect(offsets[:, 8 : 16]), val1_1[:])
-        nc.vector.tensor_copy(win0[:].indirect(offsets[:, 16 : 32]), val0_2[:])
-        nc.sync.dma_start(out=out[0 : 128, :], in_=win0[:])
-        nc.vector.tensor_copy(win1[:].indirect(offsets[:, 16 : 32]), val1_2[:])
-        nc.sync.dma_start(out=out[128 : 256, :], in_=win1[:])
+        acc = {}
+
+        def mm(name, qc, qs, a, b):
+            acc[name] = psum.tile([P, b - a], F32, name="acc" + name)
+            product(nc, acc[name][:], qc[:], qs[:], gc[:, a:b], gs[:, a:b])
+
+        def out_of_psum(name):
+            values = held.tile(acc[name].shape, F32, name="val" + name)
+            S(out=values[:], in_=acc[name][:])
+            return values[:]
+
+        nc.sync.dma_start(out=q0_raw[:], in_=qm_rows[:, :, 0:128])
+        nc.sync.dma_start(out=g0_raw[:], in_=g_rows[:, :, 0:128])
+        nc.sync.dma_start(out=g1_raw[:], in_=g_rows[:, :, 128:256])
+        nc.sync.dma_start(offsets[:], offs)
+        nc.sync.dma_start(out=q1_raw[:], in_=qm_rows[:, :, 128:256])
+        nc.sync.dma_start(out=g2_raw[:], in_=g_rows[:, :, 256:384])
+        nc.sync.dma_start(out=g3_raw[:], in_=g_rows[:, :, 384:512])
+        nc.vector.memset(win0[:, 0:8], 0.0)
+        warm = held.tile([P, 8], F32, name="warm")
+        S(out=warm[:], in_=win0[:, 0:8])
+        nc.vector.memset(win0[:, 8:T], 0.0)
+        nc.vector.memset(win1[:], 0.0)
+        q0_grp, g0_grp = grp_tile("q0", 128), grp_tile("g0", 128)
+        q1_grp, g1_grp, g2_grp, g3_grp = grp_tile("q1", 128), grp_tile("g1", 128), grp_tile("g2", 128), grp_tile("g3", 128)
+        interleave(S, q0_grp[:], q0_raw[:])
+        interleave(V, g0_grp[:], g0_raw[:])
+        quantize(nc, q0c[:], q0s[:], q0_grp[:])
+        quantize(nc, gc[:, 0:128], gs[:, 0:128], g0_grp[:])
+        mm("00", q0c, q0s, 0, 128)
+        interleave(S, g1_grp[:], g1_raw[:])
+        v00 = out_of_psum("00")
+        quantize(nc, gc[:, 128:256], gs[:, 128:256], g1_grp[:])
+        mm("01", q0c, q0s, 128, 256)
+        scatter(win0, v00, 0, 128)
+        interleave(S, q1_grp[:], q1_raw[:])
+        v01 = q1_raw[:, 0, :]
+        S(out=v01, in_=acc["01"][:])
+        quantize(nc, q1c[:], q1s[:], q1_grp[:])
+        mm("10", q1c, q1s, 0, 128)
+        mm("11", q1c, q1s, 128, 256)
+        scatter(win0, v01, 128, 256)
+        interleave(S, g2_grp[:], g2_raw[:])
+        v10 = g2_raw[:, 0, :]
+        S(out=v10, in_=acc["10"][:])
+        quantize(nc, gc[:, 256:384], gs[:, 256:384], g2_grp[:])
+        mm("02", q0c, q0s, 256, 384)
+        scatter(win1, v10, 0, 128)
+        interleave(S, g3_grp[:], g3_raw[:])
+        v02 = g3_raw[:, 0, :]
+        S(out=v02, in_=acc["02"][:])
+        v11 = g3_raw[:, 1, :]
+        S(out=v11, in_=acc["11"][:])
+        quantize(nc, gc[:, 384:512], gs[:, 384:512], g3_grp[:])
+        mm("03", q0c, q0s, 384, 512)
+        mm("1c", q1c, q1s, 256, 512)
+        scatter(win0, v02, 256, 384)
+        scatter(win1, v11, 128, 256)
+        scatter(win0, out_of_psum("03"), 384, 512)
+        nc.sync.dma_start(out=out[0:128, :], in_=win0[:])
+        scatter(win1, out_of_psum("1c"), 256, 512)
+        nc.sync.dma_start(out=out[128:256, :], in_=win1[:])

@@ -66,8 +66,8 @@ def tile_attend_dk_kernel(tc, g, qm, offs, out):
         def scatter(window, values, a, b):
             nc.vector.tensor_copy(window[:].indirect(offsets[:, a // 16 : b // 16]), values)
 
-        q0_raw, q1_raw = raw_tile("q0", 128), raw_tile("q1", 128)
-        g0_raw, g1_raw, g2_raw, g3_raw = raw_tile("g0", 128), raw_tile("g1", 128), raw_tile("g2", 128), raw_tile("g3", 128)
+        q_raw = raw_tile("q", 256)
+        g0_raw, g1_raw, g2_raw = raw_tile("g0", 128), raw_tile("g1", 128), raw_tile("g2", 256)
         q0c, q0s = mx_tiles("q0", 128)
         q1c, q1s = mx_tiles("q1", 128)
         gc, gs = mx_tiles("g", 512)
@@ -84,13 +84,11 @@ def tile_attend_dk_kernel(tc, g, qm, offs, out):
             S(out=values[:], in_=acc[name][:])
             return values[:]
 
-        nc.sync.dma_start(out=q0_raw[:], in_=qm_rows[:, :, 0:128])
+        nc.sync.dma_start(out=q_raw[:], in_=qm_rows)
         nc.sync.dma_start(out=g0_raw[:], in_=g_rows[:, :, 0:128])
         nc.sync.dma_start(out=g1_raw[:], in_=g_rows[:, :, 128:256])
         nc.sync.dma_start(offsets[:], offs)
-        nc.sync.dma_start(out=q1_raw[:], in_=qm_rows[:, :, 128:256])
-        nc.sync.dma_start(out=g2_raw[:], in_=g_rows[:, :, 256:384])
-        nc.sync.dma_start(out=g3_raw[:], in_=g_rows[:, :, 384:512])
+        nc.sync.dma_start(out=g2_raw[:], in_=g_rows[:, :, 256:512])
         nc.vector.memset(win0[:, 0:8], 0.0)
         warm = held.tile([P, 8], F32, name="warm")
         S(out=warm[:], in_=win0[:, 0:8])
@@ -98,40 +96,35 @@ def tile_attend_dk_kernel(tc, g, qm, offs, out):
         nc.vector.memset(win1[:], 0.0)
         q0_grp, g0_grp = grp_tile("q0", 128), grp_tile("g0", 128)
         q1_grp, g1_grp, g2_grp, g3_grp = grp_tile("q1", 128), grp_tile("g1", 128), grp_tile("g2", 128), grp_tile("g3", 128)
-        interleave(S, q0_grp[:], q0_raw[:])
-        interleave(V, g0_grp[:], g0_raw[:])
+        interleave(V, q0_grp[:], q_raw[:, :, 0:128])
+        interleave(S, q1_grp[:], q_raw[:, :, 128:256])
         quantize(nc, q0c[:], q0s[:], q0_grp[:])
+        interleave(V, g0_grp[:], g0_raw[:])
+        quantize(nc, q1c[:], q1s[:], q1_grp[:])
         quantize(nc, gc[:, 0:128], gs[:, 0:128], g0_grp[:])
         mm("00", q0c, q0s, 0, 128)
-        interleave(S, g1_grp[:], g1_raw[:])
+        mm("10", q1c, q1s, 0, 128)
+        interleave(V, g1_grp[:], g1_raw[:])
         v00 = out_of_psum("00")
+        v10 = out_of_psum("10")
         quantize(nc, gc[:, 128:256], gs[:, 128:256], g1_grp[:])
         mm("01", q0c, q0s, 128, 256)
-        scatter(win0, v00, 0, 128)
-        interleave(S, q1_grp[:], q1_raw[:])
-        v01 = q1_raw[:, 0, :]
-        S(out=v01, in_=acc["01"][:])
-        quantize(nc, q1c[:], q1s[:], q1_grp[:])
-        mm("10", q1c, q1s, 0, 128)
         mm("11", q1c, q1s, 128, 256)
-        scatter(win0, v01, 128, 256)
-        interleave(S, g2_grp[:], g2_raw[:])
-        v10 = g2_raw[:, 0, :]
-        S(out=v10, in_=acc["10"][:])
-        quantize(nc, gc[:, 256:384], gs[:, 256:384], g2_grp[:])
-        mm("02", q0c, q0s, 256, 384)
+        scatter(win0, v00, 0, 128)
         scatter(win1, v10, 0, 128)
-        interleave(S, g3_grp[:], g3_raw[:])
-        v02 = g3_raw[:, 0, :]
-        S(out=v02, in_=acc["02"][:])
-        v11 = g3_raw[:, 1, :]
+        interleave(S, g2_grp[:], g2_raw[:, :, 0:128])
+        v01 = g2_raw[:, 0, 0:128]
+        S(out=v01, in_=acc["01"][:])
+        quantize(nc, gc[:, 256:384], gs[:, 256:384], g2_grp[:])
+        scatter(win0, v01, 128, 256)
+        interleave(S, g3_grp[:], g2_raw[:, :, 128:256])
+        v11 = g2_raw[:, 0, 128:256]
         S(out=v11, in_=acc["11"][:])
         quantize(nc, gc[:, 384:512], gs[:, 384:512], g3_grp[:])
-        mm("03", q0c, q0s, 384, 512)
+        mm("0c", q0c, q0s, 256, 512)
         mm("1c", q1c, q1s, 256, 512)
-        scatter(win0, v02, 256, 384)
         scatter(win1, v11, 128, 256)
-        scatter(win0, out_of_psum("03"), 384, 512)
+        scatter(win0, out_of_psum("0c"), 256, 512)
         nc.sync.dma_start(out=out[0:128, :], in_=win0[:])
         scatter(win1, out_of_psum("1c"), 256, 512)
         nc.sync.dma_start(out=out[128:256, :], in_=win1[:])

@@ -67,7 +67,8 @@ def tile_attend_dk_kernel(tc, g, qm, offs, out):
             nc.vector.tensor_copy(window[:].indirect(offsets[:, a // 16 : b // 16]), values)
 
         q_raw = raw_tile("q", 256)
-        g0_raw, g1_raw, g2_raw = raw_tile("g0", 128), raw_tile("g1", 128), raw_tile("g2", 256)
+        g0_raw, g1_raw, g2_raw = raw_tile("g0", 128), raw_tile("g1", 128), raw_tile("g2", 128)
+        g3_raw = raw_tile("g3", 128)
         q0c, q0s = mx_tiles("q0", 128)
         q1c, q1s = mx_tiles("q1", 128)
         gc, gs = mx_tiles("g", 512)
@@ -88,19 +89,17 @@ def tile_attend_dk_kernel(tc, g, qm, offs, out):
         nc.sync.dma_start(out=g0_raw[:], in_=g_rows[:, :, 0:128])
         nc.sync.dma_start(out=g1_raw[:], in_=g_rows[:, :, 128:256])
         nc.sync.dma_start(offsets[:], offs)
-        nc.sync.dma_start(out=g2_raw[:], in_=g_rows[:, :, 256:512])
-        nc.vector.memset(win0[:, 0:8], 0.0)
-        warm = held.tile([P, 8], F32, name="warm")
-        S(out=warm[:], in_=win0[:, 0:8])
-        nc.vector.memset(win0[:, 8:T], 0.0)
+        nc.sync.dma_start(out=g2_raw[:], in_=g_rows[:, :, 256:384])
+        nc.sync.dma_start(out=g3_raw[:], in_=g_rows[:, :, 384:512])
+        nc.vector.memset(win0[:], 0.0)
         nc.vector.memset(win1[:], 0.0)
         q0_grp, g0_grp = grp_tile("q0", 128), grp_tile("g0", 128)
         q1_grp, g1_grp, g2_grp, g3_grp = grp_tile("q1", 128), grp_tile("g1", 128), grp_tile("g2", 128), grp_tile("g3", 128)
         interleave(V, q0_grp[:], q_raw[:, :, 0:128])
-        interleave(S, q1_grp[:], q_raw[:, :, 128:256])
+        interleave(V, q1_grp[:], q_raw[:, :, 128:256])
         quantize(nc, q0c[:], q0s[:], q0_grp[:])
-        interleave(V, g0_grp[:], g0_raw[:])
         quantize(nc, q1c[:], q1s[:], q1_grp[:])
+        interleave(V, g0_grp[:], g0_raw[:])
         quantize(nc, gc[:, 0:128], gs[:, 0:128], g0_grp[:])
         mm("00", q0c, q0s, 0, 128)
         mm("10", q1c, q1s, 0, 128)
@@ -112,15 +111,15 @@ def tile_attend_dk_kernel(tc, g, qm, offs, out):
         mm("11", q1c, q1s, 128, 256)
         scatter(win0, v00, 0, 128)
         scatter(win1, v10, 0, 128)
-        interleave(S, g2_grp[:], g2_raw[:, :, 0:128])
-        v01 = g2_raw[:, 0, 0:128]
-        S(out=v01, in_=acc["01"][:])
+        interleave(S, g2_grp[:], g2_raw[:])
         quantize(nc, gc[:, 256:384], gs[:, 256:384], g2_grp[:])
-        scatter(win0, v01, 128, 256)
-        interleave(S, g3_grp[:], g2_raw[:, :, 128:256])
-        v11 = g2_raw[:, 0, 128:256]
-        S(out=v11, in_=acc["11"][:])
+        interleave(S, g3_grp[:], g3_raw[:])
         quantize(nc, gc[:, 384:512], gs[:, 384:512], g3_grp[:])
+        v01 = g3_raw[:, 0, :]
+        S(out=v01, in_=acc["01"][:])
+        v11 = g3_raw[:, 1, :]
+        S(out=v11, in_=acc["11"][:])
+        scatter(win0, v01, 128, 256)
         mm("0c", q0c, q0s, 256, 512)
         mm("1c", q1c, q1s, 256, 512)
         scatter(win1, v11, 128, 256)

@@ -58,72 +58,105 @@ def tile_attend_dk_kernel(tc, g, qm, offs, out):
         def grp_tile(name, width, tag=""):
             return held.tile([P, width, PACK], BF16, name=name + "_grp", align_bytes=64, tag=tag)
 
-        def mx_tiles(name, width):
-            codes = held.tile([P, width], U32, name=name + "_codes", align_bytes=64)
+        def mx_tiles(name, width, tag=""):
+            codes = held.tile([P, width], U32, name=name + "_codes", align_bytes=64, tag=tag)
             scales = held.tile([P, width], U8, name=name + "_scales", align_bytes=64)
             return codes, scales
 
         def scatter(window, values, a, b):
-            nc.vector.tensor_copy(window[:].indirect(offsets[:, a // 16 : b // 16]), values)
+            nc.vector.tensor_tensor(window[:].indirect(offsets[:, a // 16 : b // 16]), values, zeros[:, 0 : b - a], mybir.AluOpType.add)
 
-        q_raw = raw_tile("q", 256)
-        g0_raw, g1_raw, g2_raw = raw_tile("g0", 128), raw_tile("g1", 128), raw_tile("g2", 128)
-        g3_raw = raw_tile("g3", 128)
-        q0c, q0s = mx_tiles("q0", 128)
-        q1c, q1s = mx_tiles("q1", 128)
-        gc, gs = mx_tiles("g", 512)
-        win0 = held.tile([P, T], F32, name="win0")
-        win1 = held.tile([P, T], F32, name="win1")
+        win = [held.tile([P, T], F32, name="win%d" % h) for h in range(2)]
+        vals = [held.tile([P, SLOTS], F32, name="vals%d" % h) for h in range(2)]
+        zeros = held.tile([P, 256], F32, name="zeros")
         acc = {}
+        qmx = [mx_tiles("q%d" % h, 128) for h in range(2)]
+        gmx = {}
+        raw = {}
+        grp = {}
+        q_raw = raw_tile("q", 256)
 
-        def mm(name, qc, qs, a, b):
-            acc[name] = psum.tile([P, b - a], F32, name="acc" + name)
-            product(nc, acc[name][:], qc[:], qs[:], gc[:, a:b], gs[:, a:b])
+        def load(k):
+            a, b = CUTS[k], CUTS[k + 1]
+            raw[k] = raw_tile("g%d" % k, b - a)
+            nc.sync.dma_start(out=raw[k][:], in_=g_rows[:, :, a:b])
 
-        def out_of_psum(name):
-            values = held.tile(acc[name].shape, F32, name="val" + name)
-            S(out=values[:], in_=acc[name][:])
-            return values[:]
+        def cast(copy, k, tag=""):
+            grp[k] = grp_tile("g%d" % k, CUTS[k + 1] - CUTS[k], tag)
+            interleave(copy, grp[k][:], raw[k][:])
 
+        def quant(k):
+            gmx[k] = mx_tiles("g%d" % k, CUTS[k + 1] - CUTS[k], "codes%d" % k)
+            quantize(nc, gmx[k][0][:], gmx[k][1][:], grp[k][:])
+
+        def mm(h, k):
+            acc[h, k] = psum.tile([P, CUTS[k + 1] - CUTS[k]], F32, name="acc%d%d" % (h, k), tag="bank%d" % (len(acc) % 8))
+            product(nc, acc[h, k][:], qmx[h][0][:], qmx[h][1][:], gmx[k][0][:], gmx[k][1][:])
+
+        def ev(h, k, copy=S):
+            copy(out=vals[h][:, CUTS[k] : CUTS[k + 1]], in_=acc[h, k][:])
+
+        def sc(h, a, b):
+            scatter(win[h], vals[h][:, a:b], a, b)
+
+        def store(h):
+            nc.sync.dma_start(out=out[128 * h : 128 * h + 128, :], in_=win[h][:])
+
+        CUTS = [0, 128, 256, 384, 512]
         nc.sync.dma_start(out=q_raw[:], in_=qm_rows)
-        nc.sync.dma_start(out=g0_raw[:], in_=g_rows[:, :, 0:128])
-        nc.sync.dma_start(out=g1_raw[:], in_=g_rows[:, :, 128:256])
+        load(0)
+        load(1)
         nc.sync.dma_start(offsets[:], offs)
-        nc.sync.dma_start(out=g2_raw[:], in_=g_rows[:, :, 256:384])
-        nc.sync.dma_start(out=g3_raw[:], in_=g_rows[:, :, 384:512])
-        nc.vector.memset(win0[:], 0.0)
-        nc.vector.memset(win1[:], 0.0)
-        q0_grp, g0_grp = grp_tile("q0", 128), grp_tile("g0", 128)
-        q1_grp, g1_grp, g2_grp, g3_grp = grp_tile("q1", 128), grp_tile("g1", 128), grp_tile("g2", 128), grp_tile("g3", 128)
+        load(2)
+        load(3)
+        nc.vector.memset(win[0][:], 0.0)
+        nc.vector.memset(win[1][:], 0.0)
+        nc.vector.memset(zeros[:], 0.0)
+        q0_grp = grp_tile("q0", 128)
+        q1_grp = grp_tile("q1", 128, "q1stage")
         interleave(V, q0_grp[:], q_raw[:, :, 0:128])
         interleave(V, q1_grp[:], q_raw[:, :, 128:256])
-        quantize(nc, q0c[:], q0s[:], q0_grp[:])
-        quantize(nc, q1c[:], q1s[:], q1_grp[:])
-        interleave(V, g0_grp[:], g0_raw[:])
-        quantize(nc, gc[:, 0:128], gs[:, 0:128], g0_grp[:])
-        mm("00", q0c, q0s, 0, 128)
-        mm("10", q1c, q1s, 0, 128)
-        interleave(V, g1_grp[:], g1_raw[:])
-        v00 = out_of_psum("00")
-        v10 = out_of_psum("10")
-        quantize(nc, gc[:, 128:256], gs[:, 128:256], g1_grp[:])
-        mm("01", q0c, q0s, 128, 256)
-        mm("11", q1c, q1s, 128, 256)
-        scatter(win0, v00, 0, 128)
-        scatter(win1, v10, 0, 128)
-        interleave(S, g2_grp[:], g2_raw[:])
-        quantize(nc, gc[:, 256:384], gs[:, 256:384], g2_grp[:])
-        interleave(S, g3_grp[:], g3_raw[:])
-        quantize(nc, gc[:, 384:512], gs[:, 384:512], g3_grp[:])
-        v01 = g3_raw[:, 0, :]
-        S(out=v01, in_=acc["01"][:])
-        v11 = g3_raw[:, 1, :]
-        S(out=v11, in_=acc["11"][:])
-        scatter(win0, v01, 128, 256)
-        mm("0c", q0c, q0s, 256, 512)
-        mm("1c", q1c, q1s, 256, 512)
-        scatter(win1, v11, 128, 256)
-        scatter(win0, out_of_psum("0c"), 256, 512)
-        nc.sync.dma_start(out=out[0:128, :], in_=win0[:])
-        scatter(win1, out_of_psum("1c"), 256, 512)
-        nc.sync.dma_start(out=out[128:256, :], in_=win1[:])
+        quantize(nc, qmx[0][0][:], qmx[0][1][:], q0_grp[:])
+        ga = grp_tile("ga", 64)
+        gb = grp_tile("gb", 64)
+        interleave(V, ga[:], raw[0][:, :, 0:64])
+        interleave(V, gb[:], raw[0][:, :, 64:128])
+        quantize(nc, qmx[1][0][:], qmx[1][1][:], q1_grp[:])
+        gmx[0] = mx_tiles("g0", 128)
+        quantize(nc, gmx[0][0][:, 0:64], gmx[0][1][:, 0:64], ga[:])
+        acc_a = psum.tile([P, 64], F32, name="acc_a", tag="first")
+        product(nc, acc_a[:], qmx[0][0][:], qmx[0][1][:], gmx[0][0][:, 0:64], gmx[0][1][:, 0:64])
+        quantize(nc, gmx[0][0][:, 64:128], gmx[0][1][:, 64:128], gb[:])
+        mm(1, 0)
+        acc_b = psum.tile([P, 64], F32, name="acc_b")
+        product(nc, acc_b[:], qmx[0][0][:], qmx[0][1][:], gmx[0][0][:, 64:128], gmx[0][1][:, 64:128])
+        cast(V, 1, "q1stage")
+        quant(1)
+        mm(0, 1)
+        mm(1, 1)
+        S(out=vals[0][:, 0:64], in_=acc_a[:])
+        sc(0, 0, 64)
+        ev(1, 0)
+        sc(1, 0, 128)
+        cast(S, 2)
+        quant(2)
+        mm(1, 2)
+        mm(0, 2)
+        S(out=vals[0][:, 64:128], in_=acc_b[:])
+        ev(0, 1)
+        sc(0, 64, 256)
+        cast(S, 3)
+        quant(3)
+        mm(0, 3)
+        acc[1, 3] = psum.tile([P, 128], F32, name="acc_z", tag="first")
+        product(nc, acc[1, 3][:], qmx[1][0][:], qmx[1][1][:], gmx[3][0][:], gmx[3][1][:])
+        ev(1, 1)
+        ev(1, 2)
+        sc(1, 128, 320)
+        ev(0, 2)
+        ev(0, 3)
+        sc(0, 256, 512)
+        store(0)
+        ev(1, 3)
+        sc(1, 320, 512)
+        store(1)

@@ -58,105 +58,115 @@ def tile_attend_dk_kernel(tc, g, qm, offs, out):
         def grp_tile(name, width, tag=""):
             return held.tile([P, width, PACK], BF16, name=name + "_grp", align_bytes=64, tag=tag)
 
-        def mx_tiles(name, width, tag=""):
+        def mx_tiles(name, width, tag="", stag=""):
             codes = held.tile([P, width], U32, name=name + "_codes", align_bytes=64, tag=tag)
-            scales = held.tile([P, width], U8, name=name + "_scales", align_bytes=64)
+            scales = held.tile([P, width], U8, name=name + "_scales", align_bytes=64, tag=stag)
             return codes, scales
 
-        def scatter(window, values, a, b):
-            nc.vector.tensor_tensor(window[:].indirect(offsets[:, a // 16 : b // 16]), values, zeros[:, 0 : b - a], mybir.AluOpType.add)
+        def val_tile(name, width, tag=""):
+            return held.tile([P, width], F32, name=name + "_vals", tag=tag)
+
+        def bank(name, width, tag=""):
+            return psum.tile([P, width], F32, name=name + "_acc", tag=tag)
 
         win = [held.tile([P, T], F32, name="win%d" % h) for h in range(2)]
-        vals = [held.tile([P, SLOTS], F32, name="vals%d" % h) for h in range(2)]
-        zeros = held.tile([P, 256], F32, name="zeros")
-        acc = {}
+        zeros = held.tile([P, 64], F32, name="zeros")
         qmx = [mx_tiles("q%d" % h, 128) for h in range(2)]
-        gmx = {}
-        raw = {}
-        grp = {}
-        q_raw = raw_tile("q", 256)
 
-        def load(k):
-            a, b = CUTS[k], CUTS[k + 1]
-            raw[k] = raw_tile("g%d" % k, b - a)
-            nc.sync.dma_start(out=raw[k][:], in_=g_rows[:, :, a:b])
+        def scatter(h, values, a, b):
+            nc.vector.tensor_tensor(win[h][:].indirect(offsets[:, a // 16 : b // 16]), values, zeros[:, 0 : b - a], mybir.AluOpType.add)
 
-        def cast(copy, k, tag=""):
-            grp[k] = grp_tile("g%d" % k, CUTS[k + 1] - CUTS[k], tag)
-            interleave(copy, grp[k][:], raw[k][:])
+        def scopy(h, values, a, b):
+            nc.vector.tensor_copy(win[h][:].indirect(offsets[:, a // 16 : b // 16]), values)
 
-        def quant(k):
-            gmx[k] = mx_tiles("g%d" % k, CUTS[k + 1] - CUTS[k], "codes%d" % k)
-            quantize(nc, gmx[k][0][:], gmx[k][1][:], grp[k][:])
+        def mm(acc, h, mx, a, b):
+            product(nc, acc, qmx[h][0][:], qmx[h][1][:], mx[0][:, a:b], mx[1][:, a:b])
 
-        def mm(h, k):
-            acc[h, k] = psum.tile([P, CUTS[k + 1] - CUTS[k]], F32, name="acc%d%d" % (h, k), tag="bank%d" % (len(acc) % 8))
-            product(nc, acc[h, k][:], qmx[h][0][:], qmx[h][1][:], gmx[k][0][:], gmx[k][1][:])
+        def quant(mx, a, b, grouped):
+            quantize(nc, mx[0][:, a:b], mx[1][:, a:b], grouped)
 
-        def ev(h, k, copy=S):
-            copy(out=vals[h][:, CUTS[k] : CUTS[k + 1]], in_=acc[h, k][:])
-
-        def sc(h, a, b):
-            scatter(win[h], vals[h][:, a:b], a, b)
+        def load(name, a, b, tag="", queue=nc.sync):
+            raw = raw_tile(name, b - a, tag)
+            queue.dma_start(out=raw[:], in_=g_rows[:, :, a:b])
+            return raw
 
         def store(h):
             nc.sync.dma_start(out=out[128 * h : 128 * h + 128, :], in_=win[h][:])
 
-        CUTS = [0, 128, 256, 384, 512]
+        q_raw = raw_tile("q", 256)
         nc.sync.dma_start(out=q_raw[:], in_=qm_rows)
-        load(0)
-        load(1)
+        raw0 = load("g0", 0, 128)
+        raw1 = load("g1", 128, 256)
         nc.sync.dma_start(offsets[:], offs)
-        load(2)
-        load(3)
+        raw2 = load("g2", 256, 384)
+        raw3 = load("g3", 384, 512)
         nc.vector.memset(win[0][:], 0.0)
         nc.vector.memset(win[1][:], 0.0)
         nc.vector.memset(zeros[:], 0.0)
-        q0_grp = grp_tile("q0", 128)
+        q0_grp = grp_tile("q0", 128, "q0stage")
         q1_grp = grp_tile("q1", 128, "q1stage")
+        ga = grp_tile("ga", 64)
+        gb = grp_tile("gb", 64)
+        mx0 = mx_tiles("g0", 128)
         interleave(V, q0_grp[:], q_raw[:, :, 0:128])
         interleave(V, q1_grp[:], q_raw[:, :, 128:256])
         quantize(nc, qmx[0][0][:], qmx[0][1][:], q0_grp[:])
-        ga = grp_tile("ga", 64)
-        gb = grp_tile("gb", 64)
-        interleave(V, ga[:], raw[0][:, :, 0:64])
-        interleave(V, gb[:], raw[0][:, :, 64:128])
+        warm = bank("warm", 64, "warm")
+        mm(warm[:], 0, qmx[0], 0, 64)
+        interleave(V, ga[:], raw0[:, :, 0:64])
+        interleave(V, gb[:], raw0[:, :, 64:128])
+        quant(mx0, 0, 64, ga[:])
+        acc_a = bank("a", 64, "first")
+        mm(acc_a[:], 0, mx0, 0, 64)
         quantize(nc, qmx[1][0][:], qmx[1][1][:], q1_grp[:])
-        gmx[0] = mx_tiles("g0", 128)
-        quantize(nc, gmx[0][0][:, 0:64], gmx[0][1][:, 0:64], ga[:])
-        acc_a = psum.tile([P, 64], F32, name="acc_a", tag="first")
-        product(nc, acc_a[:], qmx[0][0][:], qmx[0][1][:], gmx[0][0][:, 0:64], gmx[0][1][:, 0:64])
-        quantize(nc, gmx[0][0][:, 64:128], gmx[0][1][:, 64:128], gb[:])
-        mm(1, 0)
-        acc_b = psum.tile([P, 64], F32, name="acc_b")
-        product(nc, acc_b[:], qmx[0][0][:], qmx[0][1][:], gmx[0][0][:, 64:128], gmx[0][1][:, 64:128])
-        cast(V, 1, "q1stage")
-        quant(1)
-        mm(0, 1)
-        mm(1, 1)
-        S(out=vals[0][:, 0:64], in_=acc_a[:])
-        sc(0, 0, 64)
-        ev(1, 0)
-        sc(1, 0, 128)
-        cast(S, 2)
-        quant(2)
-        mm(1, 2)
-        mm(0, 2)
-        S(out=vals[0][:, 64:128], in_=acc_b[:])
-        ev(0, 1)
-        sc(0, 64, 256)
-        cast(S, 3)
-        quant(3)
-        mm(0, 3)
-        acc[1, 3] = psum.tile([P, 128], F32, name="acc_z", tag="first")
-        product(nc, acc[1, 3][:], qmx[1][0][:], qmx[1][1][:], gmx[3][0][:], gmx[3][1][:])
-        ev(1, 1)
-        ev(1, 2)
-        sc(1, 128, 320)
-        ev(0, 2)
-        ev(0, 3)
-        sc(0, 256, 512)
+        quant(mx0, 64, 128, gb[:])
+        acc10 = bank("b0", 128)
+        mm(acc10[:], 1, mx0, 0, 128)
+        acc0m = bank("am", 192)
+        mm(acc0m[:, 0:64], 0, mx0, 64, 128)
+        g1 = grp_tile("g1", 128, "q1stage")
+        mx1 = mx_tiles("g1", 128)
+        for a in (0, 64):
+            interleave(V, g1[:, a : a + 64, :], raw1[:, :, a : a + 64])
+        for a in (0, 64):
+            quant(mx1, a, a + 64, g1[:, a : a + 64, :])
+        mm(acc0m[:, 64:192], 0, mx1, 0, 128)
+        acc11 = bank("b1", 128)
+        mm(acc11[:], 1, mx1, 0, 128)
+        va = val_tile("a", 64)
+        S(out=va[:], in_=acc_a[:])
+        scatter(0, va[:], 0, 64)
+        vb0 = val_tile("b0", 128)
+        S(out=vb0[:], in_=acc10[:])
+        scopy(1, vb0[:], 0, 128)
+        g2 = grp_tile("g2", 128)
+        interleave(S, g2[:], raw2[:])
+        mx2 = mx_tiles("g2", 128)
+        quant(mx2, 0, 128, g2[:])
+        acc12 = bank("b2", 128)
+        mm(acc12[:], 1, mx2, 0, 128)
+        acc0l = bank("al", 128)
+        mm(acc0l[:, 0:128], 0, mx2, 0, 128)
+        vam = val_tile("am", 192)
+        S(out=vam[:], in_=acc0m[:])
+        scopy(0, vam[:], 64, 256)
+        g3 = grp_tile("g3", 128)
+        interleave(S, g3[:], raw3[:])
+        mx3 = mx_tiles("g3", 128)
+        quant(mx3, 0, 128, g3[:])
+        acc03 = bank("a3", 128, "warm")
+        mm(acc03[:], 0, mx3, 0, 128)
+        acc13 = bank("b3", 128, "first")
+        mm(acc13[:], 1, mx3, 0, 128)
+        vb = val_tile("bl", 384)
+        S(out=vb[:, 0:128], in_=acc11[:])
+        S(out=vb[:, 128:256], in_=acc12[:])
+        scopy(1, vb[:, 0:192], 128, 320)
+        val = val_tile("al", 256)
+        S(out=val[:, 0:128], in_=acc0l[:])
+        S(out=val[:, 128:256], in_=acc03[:])
+        scopy(0, val[:], 256, 512)
         store(0)
-        ev(1, 3)
-        sc(1, 320, 512)
+        S(out=vb[:, 256:384], in_=acc13[:])
+        scopy(1, vb[:, 192:384], 320, 512)
         store(1)

@@ -111,8 +111,6 @@ def tile_attend_dk_kernel(tc, g, qm, offs, out):
         interleave(V, q0_grp[:], q_raw[:, :, 0:128])
         interleave(V, q1_grp[:], q_raw[:, :, 128:256])
         quantize(nc, qmx[0][0][:], qmx[0][1][:], q0_grp[:])
-        warm = bank("warm", 64, "warm")
-        mm(warm[:], 0, qmx[0], 0, 64)
         interleave(V, ga[:], raw0[:, :, 0:64])
         interleave(V, gb[:], raw0[:, :, 64:128])
         quant(mx0, 0, 64, ga[:])
@@ -122,15 +120,16 @@ def tile_attend_dk_kernel(tc, g, qm, offs, out):
         quant(mx0, 64, 128, gb[:])
         acc10 = bank("b0", 128)
         mm(acc10[:], 1, mx0, 0, 128)
-        acc0m = bank("am", 192)
-        mm(acc0m[:, 0:64], 0, mx0, 64, 128)
+        acc_a2 = bank("a2", 64, "third")
+        mm(acc_a2[:], 0, mx0, 64, 128)
         g1 = grp_tile("g1", 128, "q1stage")
         mx1 = mx_tiles("g1", 128)
         for a in (0, 64):
             interleave(V, g1[:, a : a + 64, :], raw1[:, :, a : a + 64])
         for a in (0, 64):
             quant(mx1, a, a + 64, g1[:, a : a + 64, :])
-        mm(acc0m[:, 64:192], 0, mx1, 0, 128)
+        acc01 = bank("a1", 128)
+        mm(acc01[:], 0, mx1, 0, 128)
         acc11 = bank("b1", 128)
         mm(acc11[:], 1, mx1, 0, 128)
         va = val_tile("a", 64)
@@ -139,6 +138,8 @@ def tile_attend_dk_kernel(tc, g, qm, offs, out):
         vb0 = val_tile("b0", 128)
         S(out=vb0[:], in_=acc10[:])
         scopy(1, vb0[:], 0, 128)
+        vam = val_tile("am", 192)
+        S(out=vam[:, 0:64], in_=acc_a2[:])
         g2 = grp_tile("g2", 128)
         interleave(S, g2[:], raw2[:])
         mx2 = mx_tiles("g2", 128)
@@ -147,15 +148,17 @@ def tile_attend_dk_kernel(tc, g, qm, offs, out):
         mm(acc12[:], 1, mx2, 0, 128)
         acc0l = bank("al", 128)
         mm(acc0l[:, 0:128], 0, mx2, 0, 128)
-        vam = val_tile("am", 192)
-        S(out=vam[:], in_=acc0m[:])
+        S(out=vam[:, 64:192], in_=acc01[:])
         scopy(0, vam[:], 64, 256)
         g3 = grp_tile("g3", 128)
         interleave(S, g3[:], raw3[:])
         mx3 = mx_tiles("g3", 128)
-        quant(mx3, 0, 128, g3[:])
-        acc03 = bank("a3", 128, "warm")
-        mm(acc03[:], 0, mx3, 0, 128)
+        quant(mx3, 0, 64, g3[:, 0:64, :])
+        acc03 = bank("a3", 64)
+        mm(acc03[:], 0, mx3, 0, 64)
+        quant(mx3, 64, 128, g3[:, 64:128, :])
+        acc04 = bank("a4", 64, "third")
+        mm(acc04[:], 0, mx3, 64, 128)
         acc13 = bank("b3", 128, "first")
         mm(acc13[:], 1, mx3, 0, 128)
         vb = val_tile("bl", 384)
@@ -164,7 +167,8 @@ def tile_attend_dk_kernel(tc, g, qm, offs, out):
         scopy(1, vb[:, 0:192], 128, 320)
         val = val_tile("al", 256)
         S(out=val[:, 0:128], in_=acc0l[:])
-        S(out=val[:, 128:256], in_=acc03[:])
+        S(out=val[:, 128:192], in_=acc03[:])
+        S(out=val[:, 192:256], in_=acc04[:])
         scopy(0, val[:], 256, 512)
         store(0)
         S(out=vb[:, 256:384], in_=acc13[:])

@@ -53,7 +53,7 @@ def tile_attend_dk_kernel(tc, g, qm, offs, out):
         V, S = nc.vector.tensor_copy, nc.scalar.copy
 
         def raw_tile(name, width, tag=""):
-            return held.tile([P, PACK, width], F32, name=name + "_raw", tag=tag)
+            return held.tile([P, PACK, width], F32, name=name + "_raw", align_bytes=64, tag=tag)
 
         def grp_tile(name, width, tag=""):
             return held.tile([P, width, PACK], BF16, name=name + "_grp", align_bytes=64, tag=tag)
@@ -64,20 +64,19 @@ def tile_attend_dk_kernel(tc, g, qm, offs, out):
             return codes, scales
 
         def val_tile(name, width, tag=""):
-            return held.tile([P, width], F32, name=name + "_vals", tag=tag)
+            return held.tile([P, width], F32, name=name + "_vals", align_bytes=64, tag=tag)
 
         def bank(name, width, tag=""):
             return psum.tile([P, width], F32, name=name + "_acc", tag=tag)
 
         win = [held.tile([P, T], F32, name="win%d" % h) for h in range(2)]
-        zeros = held.tile([P, 64], F32, name="zeros")
         qmx = [mx_tiles("q%d" % h, 128) for h in range(2)]
 
-        def scatter(h, values, a, b):
-            nc.vector.tensor_tensor(win[h][:].indirect(offsets[:, a // 16 : b // 16]), values, zeros[:, 0 : b - a], mybir.AluOpType.add)
-
-        def scopy(h, values, a, b):
+        def vscat(h, values, a, b):
             nc.vector.tensor_copy(win[h][:].indirect(offsets[:, a // 16 : b // 16]), values)
+
+        def sscat(h, values, a, b):
+            nc.scalar.activation(win[h][:].indirect(offsets[:, a // 16 : b // 16]), values, mybir.ActivationFunctionType.Copy)
 
         def mm(acc, h, mx, a, b):
             product(nc, acc, qmx[h][0][:], qmx[h][1][:], mx[0][:, a:b], mx[1][:, a:b])
@@ -90,87 +89,76 @@ def tile_attend_dk_kernel(tc, g, qm, offs, out):
             queue.dma_start(out=raw[:], in_=g_rows[:, :, a:b])
             return raw
 
-        def store(h):
-            nc.sync.dma_start(out=out[128 * h : 128 * h + 128, :], in_=win[h][:])
+        def store(h, queue=nc.sync):
+            queue.dma_start(out=out[128 * h : 128 * h + 128, :], in_=win[h][:])
+
+        def load_over(name, a):
+            both = held.tile([P, 64 + PACK * 128], F32, name=name, align_bytes=64)
+            rows = both[:, 64:].rearrange("p (t n) -> p t n", t=PACK)
+            nc.sync.dma_start(out=rows, in_=g_rows[:, :, a : a + 128])
+            return rows, both[:, 0:128]
 
         q_raw = raw_tile("q", 256)
         nc.sync.dma_start(out=q_raw[:], in_=qm_rows)
-        raw0 = load("g0", 0, 128)
-        raw1 = load("g1", 128, 256)
+        raw = [load("g0", 0, 128)[:], load("g1", 128, 256)[:]]
         nc.sync.dma_start(offsets[:], offs)
-        raw2 = load("g2", 256, 384)
-        raw3 = load("g3", 384, 512)
+        raw2, over2 = load_over("g2", 256)
+        raw3, over3 = load_over("g3", 384)
+        raw.extend([raw2, raw3])
         nc.vector.memset(win[0][:], 0.0)
         nc.vector.memset(win[1][:], 0.0)
-        nc.vector.memset(zeros[:], 0.0)
-        q0_grp = grp_tile("q0", 128, "q0stage")
-        q1_grp = grp_tile("q1", 128, "q1stage")
-        ga = grp_tile("ga", 64)
-        gb = grp_tile("gb", 64)
-        mx0 = mx_tiles("g0", 128)
-        interleave(V, q0_grp[:], q_raw[:, :, 0:128])
-        interleave(V, q1_grp[:], q_raw[:, :, 128:256])
-        quantize(nc, qmx[0][0][:], qmx[0][1][:], q0_grp[:])
-        interleave(V, ga[:], raw0[:, :, 0:64])
-        interleave(V, gb[:], raw0[:, :, 64:128])
-        quant(mx0, 0, 64, ga[:])
-        acc_a = bank("a", 64, "first")
-        mm(acc_a[:], 0, mx0, 0, 64)
-        quantize(nc, qmx[1][0][:], qmx[1][1][:], q1_grp[:])
-        quant(mx0, 64, 128, gb[:])
-        acc10 = bank("b0", 128)
-        mm(acc10[:], 1, mx0, 0, 128)
-        acc_a2 = bank("a2", 64, "third")
-        mm(acc_a2[:], 0, mx0, 64, 128)
-        g1 = grp_tile("g1", 128, "q1stage")
-        mx1 = mx_tiles("g1", 128)
+        q_grp = [grp_tile("q%d" % h, 128) for h in range(2)]
+        grp = [grp_tile("g%d" % c, 128) for c in range(4)]
+        mx = [mx_tiles("g%d" % c, 128) for c in range(4)]
+        acc = [[bank("a%d%d" % (h, c), 128) for c in range(4)] for h in range(2)]
+
+        def cast(c, engine=V):
+            for a in (0, 64):
+                interleave(engine, grp[c][:, a : a + 64, :], raw[c][:, :, a : a + 64])
+
+        def qz(c):
+            for a in (0, 64):
+                quant(mx[c], a, a + 64, grp[c][:, a : a + 64, :])
+
+        def mms(c, order=(0, 1)):
+            for h in order:
+                mm(acc[h][c][:], h, mx[c], 0, 128)
+
         for a in (0, 64):
-            interleave(V, g1[:, a : a + 64, :], raw1[:, :, a : a + 64])
+            interleave(V, q_grp[0][:, a : a + 64, :], q_raw[:, :, a : a + 64])
+        interleave(S, q_grp[1][:], q_raw[:, :, 128:256])
         for a in (0, 64):
-            quant(mx1, a, a + 64, g1[:, a : a + 64, :])
-        acc01 = bank("a1", 128)
-        mm(acc01[:], 0, mx1, 0, 128)
-        acc11 = bank("b1", 128)
-        mm(acc11[:], 1, mx1, 0, 128)
-        va = val_tile("a", 64)
-        S(out=va[:], in_=acc_a[:])
-        scatter(0, va[:], 0, 64)
-        vb0 = val_tile("b0", 128)
-        S(out=vb0[:], in_=acc10[:])
-        scopy(1, vb0[:], 0, 128)
-        vam = val_tile("am", 192)
-        S(out=vam[:, 0:64], in_=acc_a2[:])
-        g2 = grp_tile("g2", 128)
-        interleave(S, g2[:], raw2[:])
-        mx2 = mx_tiles("g2", 128)
-        quant(mx2, 0, 128, g2[:])
-        acc12 = bank("b2", 128)
-        mm(acc12[:], 1, mx2, 0, 128)
-        acc0l = bank("al", 128)
-        mm(acc0l[:, 0:128], 0, mx2, 0, 128)
-        S(out=vam[:, 64:192], in_=acc01[:])
-        scopy(0, vam[:], 64, 256)
-        g3 = grp_tile("g3", 128)
-        interleave(S, g3[:], raw3[:])
-        mx3 = mx_tiles("g3", 128)
-        quant(mx3, 0, 64, g3[:, 0:64, :])
-        acc03 = bank("a3", 64)
-        mm(acc03[:], 0, mx3, 0, 64)
-        quant(mx3, 64, 128, g3[:, 64:128, :])
-        acc04 = bank("a4", 64, "third")
-        mm(acc04[:], 0, mx3, 64, 128)
-        acc13 = bank("b3", 128, "first")
-        mm(acc13[:], 1, mx3, 0, 128)
-        vb = val_tile("bl", 384)
-        S(out=vb[:, 0:128], in_=acc11[:])
-        S(out=vb[:, 128:256], in_=acc12[:])
-        scopy(1, vb[:, 0:192], 128, 320)
-        val = val_tile("al", 256)
-        S(out=val[:, 0:128], in_=acc0l[:])
-        S(out=val[:, 128:192], in_=acc03[:])
-        S(out=val[:, 192:256], in_=acc04[:])
-        scopy(0, val[:], 256, 512)
-        store(0)
-        S(out=vb[:, 256:384], in_=acc13[:])
-        scopy(1, vb[:, 192:384], 320, 512)
+            quant(qmx[0], a, a + 64, q_grp[0][:, a : a + 64, :])
+        cast(0)
+        quantize(nc, qmx[1][0][:], qmx[1][1][:], q_grp[1][:])
+        qz(0)
+        mms(0)
+        cast(1)
+        qz(1)
+        mms(1)
+        va0 = val_tile("a0", 128)
+        V(out=va0[:], in_=acc[0][0][:])
+        sscat(0, va0[:], 0, 128)
+        cast(2)
+        V(out=over2, in_=acc[0][1][:])
+        qz(2)
+        mms(2)
+        vb = val_tile("b", 384)
+        S(out=vb[:, 0:128], in_=acc[1][1][:])
+        sscat(0, over2, 128, 256)
+        cast(3)
+        V(out=over3, in_=acc[1][0][:])
+        qz(3)
+        mms(3)
+        va2 = val_tile("a2", 128)
+        V(out=va2[:], in_=acc[0][2][:])
+        S(out=vb[:, 128:256], in_=acc[1][2][:])
+        sscat(0, va2[:], 256, 384)
+        vscat(1, over3, 0, 128)
+        va3 = val_tile("a3", 128)
+        V(out=va3[:], in_=acc[0][3][:])
+        S(out=vb[:, 256:384], in_=acc[1][3][:])
+        sscat(0, va3[:], 384, 512)
+        store(0, nc.scalar)
+        vscat(1, vb[:], 128, 512)
         store(1)

@@ -92,18 +92,18 @@ def tile_attend_dk_kernel(tc, g, qm, offs, out):
         def store(h, queue=nc.sync):
             queue.dma_start(out=out[128 * h : 128 * h + 128, :], in_=win[h][:])
 
-        def load_over(name, a):
-            both = held.tile([P, 64 + PACK * 128], F32, name=name, align_bytes=64)
-            rows = both[:, 64:].rearrange("p (t n) -> p t n", t=PACK)
+        def load_over(name, a, ahead, width):
+            both = held.tile([P, ahead + PACK * 128], F32, name=name, align_bytes=64)
+            rows = both[:, ahead:].rearrange("p (t n) -> p t n", t=PACK)
             nc.sync.dma_start(out=rows, in_=g_rows[:, :, a : a + 128])
-            return rows, both[:, 0:128]
+            return rows, both[:, 0:width]
 
         q_raw = raw_tile("q", 256)
         nc.sync.dma_start(out=q_raw[:], in_=qm_rows)
         raw = [load("g0", 0, 128)[:], load("g1", 128, 256)[:]]
         nc.sync.dma_start(offsets[:], offs)
-        raw2, over2 = load_over("g2", 256)
-        raw3, over3 = load_over("g3", 384)
+        raw2, over2 = load_over("g2", 256, 64, 128)
+        raw3, vb = load_over("g3", 384, 192, 512)
         raw.extend([raw2, raw3])
         nc.vector.memset(win[0][:], 0.0)
         nc.vector.memset(win[1][:], 0.0)
@@ -138,27 +138,26 @@ def tile_attend_dk_kernel(tc, g, qm, offs, out):
         mms(1)
         va0 = val_tile("a0", 128)
         V(out=va0[:], in_=acc[0][0][:])
+        S(out=vb[:, 0:128], in_=acc[1][0][:])
         sscat(0, va0[:], 0, 128)
         cast(2)
         V(out=over2, in_=acc[0][1][:])
         qz(2)
         mms(2)
-        vb = val_tile("b", 384)
-        S(out=vb[:, 0:128], in_=acc[1][1][:])
         sscat(0, over2, 128, 256)
         cast(3)
-        V(out=over3, in_=acc[1][0][:])
+        V(out=vb[:, 128:256], in_=acc[1][1][:])
         qz(3)
         mms(3)
         va2 = val_tile("a2", 128)
         V(out=va2[:], in_=acc[0][2][:])
-        S(out=vb[:, 128:256], in_=acc[1][2][:])
+        V(out=vb[:, 256:384], in_=acc[1][2][:])
         sscat(0, va2[:], 256, 384)
-        vscat(1, over3, 0, 128)
+        vscat(1, vb[:, 0:160], 0, 160)
         va3 = val_tile("a3", 128)
+        V(out=vb[:, 384:512], in_=acc[1][3][:])
         V(out=va3[:], in_=acc[0][3][:])
-        S(out=vb[:, 256:384], in_=acc[1][3][:])
         sscat(0, va3[:], 384, 512)
         store(0, nc.scalar)
-        vscat(1, vb[:], 128, 512)
+        vscat(1, vb[:, 160:512], 160, 512)
         store(1)

@@ -92,19 +92,17 @@ def tile_attend_dk_kernel(tc, g, qm, offs, out):
         def store(h, queue=nc.sync):
             queue.dma_start(out=out[128 * h : 128 * h + 128, :], in_=win[h][:])
 
-        def load_over(name, a, ahead, width):
-            both = held.tile([P, ahead + PACK * 128], F32, name=name, align_bytes=64)
-            rows = both[:, ahead:].rearrange("p (t n) -> p t n", t=PACK)
-            nc.sync.dma_start(out=rows, in_=g_rows[:, :, a : a + 128])
-            return rows, both[:, 0:width]
-
         q_raw = raw_tile("q", 256)
         nc.sync.dma_start(out=q_raw[:], in_=qm_rows)
-        raw = [load("g0", 0, 128)[:], load("g1", 128, 256)[:]]
+        raw = [load("g0", 384, 512)[:], load("g1", 256, 384)[:]]
         nc.sync.dma_start(offsets[:], offs)
-        raw2, over2 = load_over("g2", 256, 64, 128)
-        raw3, vb = load_over("g3", 384, 192, 512)
-        raw.extend([raw2, raw3])
+        raw.append(load("g2", 128, 256)[:])
+        late = held.tile([P, 768], F32, name="late", align_bytes=64)
+        raw.append(late[:, 64:576].rearrange("p (t n) -> p t n", t=PACK))
+        nc.sync.dma_start(out=raw[3], in_=g_rows[:, :, 0:128])
+        vb0 = late[:, 0:128]
+        vb = late[:, 384:768]
+        va23 = late[:, 128:384]
         nc.vector.memset(win[0][:], 0.0)
         nc.vector.memset(win[1][:], 0.0)
         q_grp = [grp_tile("q%d" % h, 128) for h in range(2)]
@@ -112,12 +110,12 @@ def tile_attend_dk_kernel(tc, g, qm, offs, out):
         mx = [mx_tiles("g%d" % c, 128) for c in range(4)]
         acc = [[bank("a%d%d" % (h, c), 128) for c in range(4)] for h in range(2)]
 
-        def cast(c, engine=V):
-            for a in (0, 64):
+        def cast(c, halves=(0, 64), engine=V):
+            for a in halves:
                 interleave(engine, grp[c][:, a : a + 64, :], raw[c][:, :, a : a + 64])
 
-        def qz(c):
-            for a in (0, 64):
+        def qz(c, halves=(0, 64)):
+            for a in halves:
                 quant(mx[c], a, a + 64, grp[c][:, a : a + 64, :])
 
         def mms(c, order=(0, 1)):
@@ -137,27 +135,25 @@ def tile_attend_dk_kernel(tc, g, qm, offs, out):
         qz(1)
         mms(1)
         va0 = val_tile("a0", 128)
-        V(out=va0[:], in_=acc[0][0][:])
-        S(out=vb[:, 0:128], in_=acc[1][0][:])
-        sscat(0, va0[:], 0, 128)
+        S(out=va0[:], in_=acc[0][0][:])
+        sscat(0, va0[:], 384, 512)
+        va1 = val_tile("a1", 128)
+        S(out=va1[:], in_=acc[0][1][:])
+        S(out=vb[:, 256:384], in_=acc[1][1][:])
+        sscat(0, va1[:], 256, 384)
         cast(2)
-        V(out=over2, in_=acc[0][1][:])
         qz(2)
         mms(2)
-        sscat(0, over2, 128, 256)
         cast(3)
-        V(out=vb[:, 128:256], in_=acc[1][1][:])
+        V(out=vb0, in_=acc[1][0][:])
         qz(3)
         mms(3)
-        va2 = val_tile("a2", 128)
-        V(out=va2[:], in_=acc[0][2][:])
-        V(out=vb[:, 256:384], in_=acc[1][2][:])
-        sscat(0, va2[:], 256, 384)
-        vscat(1, vb[:, 0:160], 0, 160)
-        va3 = val_tile("a3", 128)
-        V(out=vb[:, 384:512], in_=acc[1][3][:])
-        V(out=va3[:], in_=acc[0][3][:])
-        sscat(0, va3[:], 384, 512)
+        S(out=vb[:, 128:256], in_=acc[1][2][:])
+        vscat(1, vb0, 384, 512)
+        V(out=va23[:, 128:256], in_=acc[0][2][:])
+        V(out=vb[:, 0:128], in_=acc[1][3][:])
+        V(out=va23[:, 0:128], in_=acc[0][3][:])
+        sscat(0, va23, 0, 256)
         store(0, nc.scalar)
-        vscat(1, vb[:, 160:512], 160, 512)
+        vscat(1, vb, 0, 384)
         store(1)

@@ -94,15 +94,18 @@ def tile_attend_dk_kernel(tc, g, qm, offs, out):
 
         q_raw = raw_tile("q", 256)
         nc.sync.dma_start(out=q_raw[:], in_=qm_rows)
-        raw = [load("g0", 384, 512)[:], load("g1", 256, 384)[:]]
+        raw = [load("g0", 0, 128)[:], load("g1", 128, 256)[:]]
         nc.sync.dma_start(offsets[:], offs)
-        raw.append(load("g2", 128, 256)[:])
-        late = held.tile([P, 768], F32, name="late", align_bytes=64)
+        mid = held.tile([P, 576], F32, name="mid", align_bytes=64)
+        raw.append(mid[:, 64:576].rearrange("p (t n) -> p t n", t=PACK))
+        nc.sync.dma_start(out=raw[2], in_=g_rows[:, :, 256:384])
+        late = held.tile([P, 640], F32, name="late", align_bytes=64)
         raw.append(late[:, 64:576].rearrange("p (t n) -> p t n", t=PACK))
-        nc.sync.dma_start(out=raw[3], in_=g_rows[:, :, 0:128])
-        vb0 = late[:, 0:128]
-        vb = late[:, 384:768]
+        nc.sync.dma_start(out=raw[3], in_=g_rows[:, :, 384:512])
+        vb0 = mid[:, 0:128]
+        va1 = late[:, 0:128]
         va23 = late[:, 128:384]
+        vb12 = late[:, 384:640]
         nc.vector.memset(win[0][:], 0.0)
         nc.vector.memset(win[1][:], 0.0)
         q_grp = [grp_tile("q%d" % h, 128) for h in range(2)]
@@ -136,24 +139,25 @@ def tile_attend_dk_kernel(tc, g, qm, offs, out):
         mms(1)
         va0 = val_tile("a0", 128)
         S(out=va0[:], in_=acc[0][0][:])
-        sscat(0, va0[:], 384, 512)
-        va1 = val_tile("a1", 128)
-        S(out=va1[:], in_=acc[0][1][:])
-        S(out=vb[:, 256:384], in_=acc[1][1][:])
-        sscat(0, va1[:], 256, 384)
+        sscat(0, va0[:], 0, 128)
         cast(2)
+        V(out=vb0, in_=acc[1][0][:])
         qz(2)
         mms(2)
+        sscat(1, vb0, 0, 128)
         cast(3)
-        V(out=vb0, in_=acc[1][0][:])
+        V(out=va1, in_=acc[0][1][:])
         qz(3)
         mms(3)
-        S(out=vb[:, 128:256], in_=acc[1][2][:])
-        vscat(1, vb0, 384, 512)
-        V(out=va23[:, 128:256], in_=acc[0][2][:])
-        V(out=vb[:, 0:128], in_=acc[1][3][:])
-        V(out=va23[:, 0:128], in_=acc[0][3][:])
-        sscat(0, va23, 0, 256)
-        store(0, nc.scalar)
-        vscat(1, vb, 0, 384)
+        V(out=vb12[:, 0:128], in_=acc[1][1][:])
+        V(out=va23[:, 0:128], in_=acc[0][2][:])
+        S(out=vb12[:, 128:256], in_=acc[1][2][:])
+        vscat(0, va1, 128, 256)
+        sscat(1, vb12, 128, 384)
+        vb3 = val_tile("b3", 128)
+        V(out=va23[:, 128:256], in_=acc[0][3][:])
+        V(out=vb3[:], in_=acc[1][3][:])
+        vscat(0, va23, 256, 512)
+        store(0)
+        vscat(1, vb3[:], 384, 512)
         store(1)

@@ -94,70 +94,65 @@ def tile_attend_dk_kernel(tc, g, qm, offs, out):
 
         q_raw = raw_tile("q", 256)
         nc.sync.dma_start(out=q_raw[:], in_=qm_rows)
-        raw = [load("g0", 0, 128)[:], load("g1", 128, 256)[:]]
+        first = load("g0", 0, 128)
+        wide = load("g12", 128, 384)
         nc.sync.dma_start(offsets[:], offs)
-        mid = held.tile([P, 576], F32, name="mid", align_bytes=64)
-        raw.append(mid[:, 64:576].rearrange("p (t n) -> p t n", t=PACK))
-        nc.sync.dma_start(out=raw[2], in_=g_rows[:, :, 256:384])
-        late = held.tile([P, 640], F32, name="late", align_bytes=64)
-        raw.append(late[:, 64:576].rearrange("p (t n) -> p t n", t=PACK))
-        nc.sync.dma_start(out=raw[3], in_=g_rows[:, :, 384:512])
-        vb0 = mid[:, 0:128]
-        va1 = late[:, 0:128]
-        va23 = late[:, 128:384]
-        vb12 = late[:, 384:640]
+        last = load("g3", 384, 512)
+        raw = [first[:], wide[:, :, 0:128], wide[:, :, 128:256], last[:]]
         nc.vector.memset(win[0][:], 0.0)
         nc.vector.memset(win[1][:], 0.0)
-        q_grp = [grp_tile("q%d" % h, 128) for h in range(2)]
-        grp = [grp_tile("g%d" % c, 128) for c in range(4)]
-        mx = [mx_tiles("g%d" % c, 128) for c in range(4)]
-        acc = [[bank("a%d%d" % (h, c), 128) for c in range(4)] for h in range(2)]
+        q0_grp = grp_tile("q0", 128)
+        g0_grp = grp_tile("g0", 128)
+        stage = grp_tile("stage", 256)
+        q1_grp = stage[:, 64:192, :]
+        grp = [g0_grp[:], stage[:, 0:128, :], stage[:, 128:256, :], stage[:, 0:128, :]]
+        mx = mx_tiles("g", 512)
+        acc_a = [bank("a%d" % c, 128) for c in range(4)]
+        b0, b12, b3 = bank("b0", 128), bank("b12", 256), bank("b3", 128)
+        va0, va1, va23 = val_tile("a0", 128), val_tile("a1", 128), val_tile("a23", 256)
+        vb0, vb = val_tile("b0", 128), val_tile("b123", 384)
 
-        def cast(c, halves=(0, 64), engine=V):
-            for a in halves:
-                interleave(engine, grp[c][:, a : a + 64, :], raw[c][:, :, a : a + 64])
+        def cast(c, a=0, width=128):
+            interleave(V, grp[c][:, a : a + width, :], raw[c][:, :, a : a + width])
 
-        def qz(c, halves=(0, 64)):
-            for a in halves:
-                quant(mx[c], a, a + 64, grp[c][:, a : a + 64, :])
-
-        def mms(c, order=(0, 1)):
-            for h in order:
-                mm(acc[h][c][:], h, mx[c], 0, 128)
+        def qz(c, a=0, width=128):
+            quant(mx, 128 * c + a, 128 * c + a + width, grp[c][:, a : a + width, :])
 
         for a in (0, 64):
-            interleave(V, q_grp[0][:, a : a + 64, :], q_raw[:, :, a : a + 64])
-        interleave(S, q_grp[1][:], q_raw[:, :, 128:256])
+            interleave(V, q0_grp[:, a : a + 64, :], q_raw[:, :, a : a + 64])
+        interleave(S, q1_grp, q_raw[:, :, 128:256])
         for a in (0, 64):
-            quant(qmx[0], a, a + 64, q_grp[0][:, a : a + 64, :])
-        cast(0)
-        quantize(nc, qmx[1][0][:], qmx[1][1][:], q_grp[1][:])
-        qz(0)
-        mms(0)
-        cast(1)
-        qz(1)
-        mms(1)
-        va0 = val_tile("a0", 128)
-        S(out=va0[:], in_=acc[0][0][:])
+            quant(qmx[0], a, a + 64, q0_grp[:, a : a + 64, :])
+        for a in (0, 64):
+            cast(0, a, 64)
+        for a in (0, 64):
+            qz(0, a, 64)
+        quantize(nc, qmx[1][0][:], qmx[1][1][:], q1_grp)
+        mm(acc_a[0][:], 0, mx, 0, 128)
+        mm(b0[:], 1, mx, 0, 128)
+        S(out=va0[:], in_=acc_a[0][:])
         sscat(0, va0[:], 0, 128)
+        cast(1)
         cast(2)
-        V(out=vb0, in_=acc[1][0][:])
+        qz(1)
+        mm(acc_a[1][:], 0, mx, 128, 256)
+        V(out=vb0[:], in_=b0[:])
+        sscat(1, vb0[:], 0, 128)
         qz(2)
-        mms(2)
-        sscat(1, vb0, 0, 128)
+        mm(b12[:], 1, mx, 128, 384)
+        mm(acc_a[2][:], 0, mx, 256, 384)
+        S(out=vb[:, 0:256], in_=b12[:])
+        S(out=va23[:, 0:128], in_=acc_a[2][:])
+        sscat(1, vb[:, 0:224], 128, 352)
         cast(3)
-        V(out=va1, in_=acc[0][1][:])
+        V(out=va1[:], in_=acc_a[1][:])
         qz(3)
-        mms(3)
-        V(out=vb12[:, 0:128], in_=acc[1][1][:])
-        V(out=va23[:, 0:128], in_=acc[0][2][:])
-        S(out=vb12[:, 128:256], in_=acc[1][2][:])
-        vscat(0, va1, 128, 256)
-        sscat(1, vb12, 128, 384)
-        vb3 = val_tile("b3", 128)
-        V(out=va23[:, 128:256], in_=acc[0][3][:])
-        V(out=vb3[:], in_=acc[1][3][:])
-        vscat(0, va23, 256, 512)
+        mm(acc_a[3][:], 0, mx, 384, 512)
+        mm(b3[:], 1, mx, 384, 512)
+        vscat(0, va1[:], 128, 256)
+        V(out=va23[:, 128:256], in_=acc_a[3][:])
+        V(out=vb[:, 256:384], in_=b3[:])
+        vscat(0, va23[:], 256, 512)
         store(0)
-        vscat(1, vb3[:], 384, 512)
+        vscat(1, vb[:, 224:384], 352, 512)
         store(1)

@@ -94,62 +94,66 @@ def tile_attend_dk_kernel(tc, g, qm, offs, out):
 
         q_raw = raw_tile("q", 256)
         nc.sync.dma_start(out=q_raw[:], in_=qm_rows)
-        first = load("g0", 0, 128)
-        wide = load("g12", 128, 384)
+        raw = [load("g0", 0, 128)[:], load("g1", 128, 256)[:]]
         nc.sync.dma_start(offsets[:], offs)
-        last = load("g3", 384, 512)
-        raw = [first[:], wide[:, :, 0:128], wide[:, :, 128:256], last[:]]
+        third = held.tile([P, 512], F32, name="third", align_bytes=64)
+        raw.append(third[:].rearrange("p (t n) -> p t n", t=PACK))
+        nc.sync.dma_start(out=raw[2], in_=g_rows[:, :, 256:384])
+        raw.append(load("g3", 384, 512)[:])
         nc.vector.memset(win[0][:], 0.0)
         nc.vector.memset(win[1][:], 0.0)
-        q0_grp = grp_tile("q0", 128)
-        g0_grp = grp_tile("g0", 128)
-        stage = grp_tile("stage", 256)
-        q1_grp = stage[:, 64:192, :]
-        grp = [g0_grp[:], stage[:, 0:128, :], stage[:, 128:256, :], stage[:, 0:128, :]]
+        q_grp = [grp_tile("q%d" % h, 128) for h in range(2)]
+        staged = held.tile([P, 256], F32, name="staged", align_bytes=64)
+        grp = [grp_tile("g%d" % c, 128)[:] for c in range(2)]
+        grp.append(staged[:].bitcast(BF16).rearrange("p (c t) -> p c t", t=PACK))
+        grp.append(third[:, 0:256].bitcast(BF16).rearrange("p (c t) -> p c t", t=PACK))
         mx = mx_tiles("g", 512)
         acc_a = [bank("a%d" % c, 128) for c in range(4)]
         b0, b12, b3 = bank("b0", 128), bank("b12", 256), bank("b3", 128)
-        va0, va1, va23 = val_tile("a0", 128), val_tile("a1", 128), val_tile("a23", 256)
+        va0, va1, va23 = val_tile("a0", 128), staged[:, 128:256], val_tile("a23", 256)
         vb0, vb = val_tile("b0", 128), val_tile("b123", 384)
 
-        def cast(c, a=0, width=128):
-            interleave(V, grp[c][:, a : a + width, :], raw[c][:, :, a : a + width])
+        def cast(c, a, width, engine=V):
+            interleave(engine, grp[c][:, a : a + width, :], raw[c][:, :, a : a + width])
 
-        def qz(c, a=0, width=128):
+        def qz(c, a, width):
             quant(mx, 128 * c + a, 128 * c + a + width, grp[c][:, a : a + width, :])
 
         for a in (0, 64):
-            interleave(V, q0_grp[:, a : a + 64, :], q_raw[:, :, a : a + 64])
-        interleave(S, q1_grp, q_raw[:, :, 128:256])
+            interleave(V, q_grp[0][:, a : a + 64, :], q_raw[:, :, a : a + 64])
+        interleave(S, q_grp[1][:], q_raw[:, :, 128:256])
         for a in (0, 64):
-            quant(qmx[0], a, a + 64, q0_grp[:, a : a + 64, :])
+            quant(qmx[0], a, a + 64, q_grp[0][:, a : a + 64, :])
         for a in (0, 64):
             cast(0, a, 64)
         for a in (0, 64):
             qz(0, a, 64)
-        quantize(nc, qmx[1][0][:], qmx[1][1][:], q1_grp)
         mm(acc_a[0][:], 0, mx, 0, 128)
+        cast(1, 0, 112)
+        cast(1, 112, 16, S)
+        quantize(nc, qmx[1][0][:], qmx[1][1][:], q_grp[1][:])
         mm(b0[:], 1, mx, 0, 128)
+        qz(1, 0, 128)
+        mm(acc_a[1][:], 0, mx, 128, 256)
         S(out=va0[:], in_=acc_a[0][:])
         sscat(0, va0[:], 0, 128)
-        cast(1)
-        cast(2)
-        qz(1)
-        mm(acc_a[1][:], 0, mx, 128, 256)
+        for a in (0, 64):
+            cast(2, a, 64)
         V(out=vb0[:], in_=b0[:])
         sscat(1, vb0[:], 0, 128)
-        qz(2)
-        mm(b12[:], 1, mx, 128, 384)
+        for a in (0, 64):
+            qz(2, a, 64)
         mm(acc_a[2][:], 0, mx, 256, 384)
-        S(out=vb[:, 0:256], in_=b12[:])
+        mm(b12[:], 1, mx, 128, 384)
         S(out=va23[:, 0:128], in_=acc_a[2][:])
+        S(out=vb[:, 0:256], in_=b12[:])
         sscat(1, vb[:, 0:224], 128, 352)
-        cast(3)
-        V(out=va1[:], in_=acc_a[1][:])
-        qz(3)
+        cast(3, 0, 128)
+        V(out=va1, in_=acc_a[1][:])
+        qz(3, 0, 128)
         mm(acc_a[3][:], 0, mx, 384, 512)
         mm(b3[:], 1, mx, 384, 512)
-        vscat(0, va1[:], 128, 256)
+        vscat(0, va1, 128, 256)
         V(out=va23[:, 128:256], in_=acc_a[3][:])
         V(out=vb[:, 256:384], in_=b3[:])
         vscat(0, va23[:], 256, 512)

from contextlib import ExitStack

import concourse.mybir as mybir

F32 = mybir.dt.float32
BF16 = mybir.dt.bfloat16
U32 = mybir.dt.uint32
U16 = mybir.dt.uint16
U8 = mybir.dt.uint8
FP8X4 = mybir.dt.float8_e4m3fn_x4

P = 128
PACK = 4
NQ = 512
SLOTS = 512
D = 256
T = 1024

FLOPS = 2 * NQ * SLOTS * D


def interleave(copy, grouped, raw):
    copy(
        out=grouped.rearrange("p (c i) t -> p c t i", i=4),
        in_=raw.rearrange("p t (c i) -> p c t i", i=4),
    )


def quantize(nc, codes, scales, grouped):
    nc.vector.quantize_mx(out=codes.bitcast(FP8X4), scales=scales, in_=grouped.rearrange("p c t -> p (c t)"))


def product(nc, acc, q_codes, q_scales, g_codes, g_scales):
    nc.tensor.matmul_mx(
        out=acc,
        lhsT=q_codes.bitcast(FP8X4),
        lhsT_scale=q_scales,
        rhs=g_codes.bitcast(FP8X4),
        rhs_scale=g_scales,
        start=True,
        stop=True,
    )


def tile_attend_dk_kernel(tc, g, qm, offs, out):
    nc = tc.nc
    g_rows = g.rearrange("b (p t) n -> p (b t) n", t=PACK)
    qm_rows = qm.rearrange("b (p t) d -> p (b t) d", t=PACK)
    with ExitStack() as ctx:
        held = ctx.enter_context(tc.tile_pool(name="held", bufs=1))
        psum = ctx.enter_context(tc.psum_pool(name="psum", bufs=1))
        offsets = held.tile([P, SLOTS // 16], U16, name="offsets")
        V, S = nc.vector.tensor_copy, nc.scalar.copy

        def raw_tile(name, width, tag=""):
            return held.tile([P, PACK, width], F32, name=name + "_raw", align_bytes=64, tag=tag)

        def grp_tile(name, width, tag=""):
            return held.tile([P, width, PACK], BF16, name=name + "_grp", align_bytes=64, tag=tag)

        def mx_tiles(name, width, tag="", stag=""):
            codes = held.tile([P, width], U32, name=name + "_codes", align_bytes=64, tag=tag)
            scales = held.tile([P, width], U8, name=name + "_scales", align_bytes=64, tag=stag)
            return codes, scales

        def val_tile(name, width, tag=""):
            return held.tile([P, width], F32, name=name + "_vals", align_bytes=64, tag=tag)

        def bank(name, width, tag=""):
            return psum.tile([P, width], F32, name=name + "_acc", tag=tag)

        win = [held.tile([P, T], F32, name="win%d" % h) for h in range(2)]
        qmx = [mx_tiles("q%d" % h, 128) for h in range(2)]

        def vscat(h, values, a, b):
            nc.vector.tensor_copy(win[h][:].indirect(offsets[:, a // 16 : b // 16]), values)

        def sscat(h, values, a, b):
            nc.scalar.activation(win[h][:].indirect(offsets[:, a // 16 : b // 16]), values, mybir.ActivationFunctionType.Copy)

        def mm(acc, h, mx, a, b):
            product(nc, acc, qmx[h][0][:], qmx[h][1][:], mx[0][:, a:b], mx[1][:, a:b])

        def quant(mx, a, b, grouped):
            quantize(nc, mx[0][:, a:b], mx[1][:, a:b], grouped)

        def load(name, a, b, tag="", queue=nc.sync):
            raw = raw_tile(name, b - a, tag)
            queue.dma_start(out=raw[:], in_=g_rows[:, :, a:b])
            return raw

        def store(h, queue=nc.sync):
            queue.dma_start(out=out[128 * h : 128 * h + 128, :], in_=win[h][:])

        q_raw = raw_tile("q", 256)
        nc.sync.dma_start(out=q_raw[:], in_=qm_rows)
        raw = [load("g0", 0, 128)[:], load("g1", 128, 256)[:]]
        nc.sync.dma_start(offsets[:], offs)
        third = held.tile([P, 512], F32, name="third", align_bytes=64)
        raw.append(third[:].rearrange("p (t n) -> p t n", t=PACK))
        nc.sync.dma_start(out=raw[2], in_=g_rows[:, :, 256:384])
        raw.append(load("g3", 384, 512)[:])
        nc.vector.memset(win[0][:], 0.0)
        nc.vector.memset(win[1][:], 0.0)
        q_grp = [grp_tile("q%d" % h, 128) for h in range(2)]
        staged = held.tile([P, 256], F32, name="staged", align_bytes=64)
        grp = [grp_tile("g%d" % c, 128)[:] for c in range(2)]
        grp.append(staged[:].bitcast(BF16).rearrange("p (c t) -> p c t", t=PACK))
        grp.append(third[:, 0:256].bitcast(BF16).rearrange("p (c t) -> p c t", t=PACK))
        mx = mx_tiles("g", 512)
        acc_a = [bank("a%d" % c, 128) for c in range(4)]
        b0, b12, b3 = bank("b0", 128), bank("b12", 256), bank("b3", 128)
        va0, va1, va23 = val_tile("a0", 128), staged[:, 128:256], val_tile("a23", 256)
        vb0, vb = val_tile("b0", 128), val_tile("b123", 384)

        def cast(c, a, width, engine=V):
            interleave(engine, grp[c][:, a : a + width, :], raw[c][:, :, a : a + width])

        def qz(c, a, width):
            quant(mx, 128 * c + a, 128 * c + a + width, grp[c][:, a : a + width, :])

        for a in (0, 64):
            interleave(V, q_grp[0][:, a : a + 64, :], q_raw[:, :, a : a + 64])
        interleave(S, q_grp[1][:], q_raw[:, :, 128:256])
        for a in (0, 64):
            quant(qmx[0], a, a + 64, q_grp[0][:, a : a + 64, :])
        for a in (0, 64):
            cast(0, a, 64)
        for a in (0, 64):
            qz(0, a, 64)
        mm(acc_a[0][:], 0, mx, 0, 128)
        cast(1, 0, 112)
        cast(1, 112, 16, S)
        quantize(nc, qmx[1][0][:], qmx[1][1][:], q_grp[1][:])
        mm(b0[:], 1, mx, 0, 128)
        qz(1, 0, 128)
        mm(acc_a[1][:], 0, mx, 128, 256)
        S(out=va0[:], in_=acc_a[0][:])
        sscat(0, va0[:], 0, 128)
        for a in (0, 64):
            cast(2, a, 64)
        V(out=vb0[:], in_=b0[:])
        sscat(1, vb0[:], 0, 128)
        for a in (0, 64):
            qz(2, a, 64)
        mm(acc_a[2][:], 0, mx, 256, 384)
        mm(b12[:], 1, mx, 128, 384)
        S(out=va23[:, 0:128], in_=acc_a[2][:])
        S(out=vb[:, 0:256], in_=b12[:])
        sscat(1, vb[:, 0:224], 128, 352)
        cast(3, 0, 128)
        V(out=va1, in_=acc_a[1][:])
        qz(3, 0, 128)
        mm(acc_a[3][:], 0, mx, 384, 512)
        mm(b3[:], 1, mx, 384, 512)
        vscat(0, va1, 128, 256)
        V(out=va23[:, 128:256], in_=acc_a[3][:])
        V(out=vb[:, 256:384], in_=b3[:])
        vscat(0, va23[:], 256, 512)
        store(0)
        vscat(1, vb[:, 224:384], 352, 512)
        store(1)
